import numpy as np
import ml_dtypes


def mxq(x, axis, fmt="e4m3"):
    dtype, down = {"e4m3": (ml_dtypes.float8_e4m3fn, 7), "e5m2": (ml_dtypes.float8_e5m2, 14)}[fmt]
    v = np.moveaxis(np.asarray(x, np.float32).astype(ml_dtypes.bfloat16).astype(np.float64), axis, -1)
    blocks = v.reshape(v.shape[:-1] + (-1, 32))
    amax = np.abs(blocks).max(-1, keepdims=True)
    byte = np.maximum(np.where(amax > 0, np.frexp(amax)[1] - 1 + 127, 0) - down, 1)
    scale = np.exp2(byte - 127.0)
    codes = (blocks / scale).astype(np.float32).astype(dtype).astype(np.float64)
    return np.moveaxis((codes * scale).reshape(v.shape), -1, axis)


WIDE = False


def mx_kscale(k):
    if not WIDE:
        return np.ones(k)
    levels = np.array([10, -10, 5, -5, 0])
    if k % 512:
        return np.exp2(np.random.permutation(np.resize(levels, k // 32))).repeat(32)
    a = np.empty((k // 512, 16))
    for p in range(k // 512):
        a[p, :8] = np.random.permutation(np.resize(levels, 8))
        for g in range(8):
            far = levels[np.abs(levels - a[p, g]) >= 10]
            a[p, g + 8] = far[np.random.randint(len(far))]
    return np.exp2(a.ravel()).repeat(32)


def f64(x):
    return np.asarray(x).astype(np.float64)


def striped(idx):
    return np.tile(idx.reshape(-1, 16).T, (8, 1)).astype(np.uint16)


def unstriped(offs):
    return offs[:16].T.reshape(-1).astype(np.int64)


E2M1 = np.array([0.0, 0.5, 1.0, 1.5, 2.0, 3.0, 4.0, 6.0, -0.0, -0.5, -1.0, -1.5, -2.0, -3.0, -4.0, -6.0])


def pack_weight(w, fmt):
    k, n = w.shape
    w = f64(np.asarray(w, np.float32).astype(ml_dtypes.bfloat16)).reshape(k // 32, 32, n)
    amax = np.abs(w).max(1)
    if fmt == "e4m3":
        byte = np.frexp(amax)[1] - 1 + 127 - 7
    else:
        mant, ex = np.frexp(amax / 6.0)
        byte = np.where(mant > 0.5, ex, ex - 1) + 127
    byte = np.clip(np.where(amax > 0, byte, 1), 1, 254)
    scaled = (w * np.exp2(127.0 - byte)[:, None, :]).reshape(k, n).astype(np.float32)
    by_word = np.ascontiguousarray(scaled.reshape(k // 512, 128, 4, n).transpose(0, 1, 3, 2))
    if fmt == "e4m3":
        words = by_word.astype(ml_dtypes.float8_e4m3fn).view(np.uint8)
    else:
        c = by_word.astype(ml_dtypes.float4_e2m1fn).view(np.uint8) & 0xF
        words = (c[..., 0::2] | (c[..., 1::2] << 4)).reshape(k // 512, 128, 2 * n)
    return np.ascontiguousarray(words), np.ascontiguousarray(byte.astype(np.uint8).reshape(k // 512, 16, n))


def unpack_weight(words, scales, fmt):
    g, _, n = scales.shape
    words = np.ascontiguousarray(words).reshape(g, 128, n, -1)
    if fmt == "e4m3":
        vals = words.view(ml_dtypes.float8_e4m3fn).astype(np.float64)
    else:
        nib = np.empty((g, 128, n, 4), np.uint8)
        nib[..., 0::2] = words & 0xF
        nib[..., 1::2] = words >> 4
        vals = E2M1[nib]
    vals = vals * np.repeat(np.exp2(scales.astype(np.float64) - 127.0), 8, axis=1)[..., None]
    return vals.transpose(0, 1, 3, 2).reshape(g * 512, n)


def gelu(v):
    return 0.5 * v * (1.0 + np.tanh(np.sqrt(2.0 / np.pi) * (v + 0.044715 * v**3)))


def striped8(idx):
    return np.concatenate([v.reshape(-1, 16).T for v in idx]).astype(np.uint16)


def unstriped8(offs):
    return np.stack([offs[16 * g:16 * g + 16].T.reshape(-1) for g in range(8)]).astype(np.int64)


def heads(xT, wgt, idx8):
    k = np.arange(xT.shape[0])
    return wgt[k // 4 % 128] * xT[k[:, None], idx8[k % 512 // 64]]


K, T, S, H, P, G = 1024, 2048, 1024, 512, 128, 8

def setup_inputs():
    n = np.random.standard_normal
    s = mx_kscale(K)[:, None]
    u = mx_kscale(H)[:, None]
    a = H ** -0.25
    ws = a * n((K, H)) / np.sqrt(K) / s * u.T
    ws_words, ws_scales = pack_weight(ws, "e2m1")
    wt = a * n((K, H)) / np.sqrt(K) / s / u.T
    return {
        "xT": (n((K, T)) * s).astype(np.float32),
        "wgt": np.repeat(np.random.uniform(0.5, 2.0, (G, S)), P // G, axis=0).astype(np.float32),
        "offs": striped8(np.stack([np.random.permutation(T)[:S] for _ in range(G)])),
        "ws_words": ws_words,
        "ws_scales": ws_scales,
        "wt": wt.astype(np.float32),
        "bs": (0.1 * n(H) * u[:, 0]).astype(np.float32),
        "bt": (0.1 * n(H) / u[:, 0]).astype(np.float32),
        "rel": np.random.uniform(0.5, 1.5, H).astype(np.float32),
    }

def reference(xT, wgt, offs, ws_words, ws_scales, wt, bs, bt, rel):
    xg = mxq(heads(f64(xT), f64(wgt), unstriped8(offs)), 0, "e4m3")
    ws = unpack_weight(ws_words, ws_scales, "e2m1")
    wtq = mxq(f64(wt), 0, "e4m3")
    hs = (ws.T @ xg) + f64(bs)[:, None]
    ht = ((wtq.T @ xg) + f64(bt)[:, None]) * f64(rel)[:, None]
    hsq = mxq(hs, 0, "e4m3")
    htq = mxq(ht, 0, "e4m3")
    y = hsq.T @ htq
    return np.maximum(y, 0.0)

@@ -1,0 +1,264 @@
+from contextlib import ExitStack
+
+import concourse.mybir as mybir
+from concourse.masks import make_identity
+
+K, T, S, H = 1024, 2048, 1024, 512
+P = 128
+PACK = 4
+K_PASS = P * PACK
+PASSES = K // K_PASS
+RUN = 8
+BLOCKS = H // (PACK * RUN)
+HALF = S // 2
+FLOPS = 2 * K * H * S * 2 + 2 * H * S * S
+
+F32 = mybir.dt.float32
+BF16 = mybir.dt.bfloat16
+I32 = mybir.dt.int32
+U32 = mybir.dt.uint32
+U16 = mybir.dt.uint16
+U8 = mybir.dt.uint8
+FP8X4 = mybir.dt.float8_e4m3fn_x4
+FP4X4 = mybir.dt.float4_e2m1fn_x4
+MULT = mybir.AluOpType.mult
+MAX = mybir.AluOpType.max
+IDENTITY = mybir.ActivationFunctionType.Identity
+RELU = mybir.ActivationFunctionType.Relu
+
+
+def tile_list_relation_pair_scores_kernel(tc, xT, wgt, offs, ws_words, ws_scales, wt, bs, bt, rel, out):
+    nc = tc.nc
+    with ExitStack() as ctx:
+        keep = ctx.enter_context(tc.tile_pool(name="keep", bufs=1))
+        stage = ctx.enter_context(tc.tile_pool(name="stage", bufs=6))
+        psum = ctx.enter_context(tc.psum_pool(name="psum", bufs=8))
+
+        def held(name, shape, dtype):
+            return keep.tile(shape, dtype, name=name, align_bytes=64)
+
+        def bank(name):
+            return psum.tile([P, HALF], F32, name=name, tag="bank")
+
+        offsets = keep.tile([P, S // 16], U16, name="offsets")
+        nc.sync.dma_start(offsets[:], offs)
+        planes = [[held("plane%d%d" % (a, i), [P, T], F32) for i in range(PACK)] for a in range(PASSES)]
+        weights = [held("weights%d" % h, [P, HALF], F32) for h in range(2)]
+        ws_raw = held("ws_raw", [P, PASSES, 2 * H // 4], I32)
+        wt_raw = [held("wt_raw%d" % a, [P, PACK, H], F32) for a in range(PASSES)]
+
+        def load_plane(a, i):
+            nc.sync.dma_start(planes[a][i][:], xT[a * K_PASS + i : (a + 1) * K_PASS : PACK, :])
+
+        ws_scale_raw = held("ws_scale_raw", [P, PASSES, H // 4], I32)
+        nc.vector.memset(ws_scale_raw[:], 0)
+        rows = held("rows", [P, P], F32)
+        nc.vector.memset(rows[:], 0.0)
+        identity = held("identity", [P, P], F32)
+        make_identity(nc, identity[:])
+
+        def load_scales(q):
+            nc.sync.dma_start(
+                ws_scale_raw[32 * q : 32 * q + 4, :, :],
+                ws_scales[:, 4 * q : 4 * q + 4, :].rearrange("a q c -> q a c").bitcast(I32),
+            )
+
+        def load_vector(v, vec):
+            nc.sync.dma_start(
+                rows[PACK * v : PACK * (v + 1), :].rearrange("t (b e) -> t b e", e=RUN),
+                vec.rearrange("(b t e) -> t b e", t=PACK, e=RUN),
+            )
+
+        load_plane(0, 0)
+        for h in range(2):
+            nc.sync.dma_start(weights[h][:], wgt[:, h * HALF : (h + 1) * HALF])
+        for i in range(1, PACK):
+            load_plane(0, i)
+            load_scales(i - 1)
+        load_scales(3)
+        nc.sync.dma_start(ws_raw[:], ws_words.rearrange("a p c -> p a c").bitcast(I32))
+        for i, vec in enumerate((bs, bt, rel)):
+            load_plane(1, i)
+            load_vector(i, vec)
+        load_plane(1, 3)
+        for a in range(PASSES):
+            nc.sync.dma_start(wt_raw[a][:], wt[a * K_PASS : (a + 1) * K_PASS, :].rearrange("(p j) c -> p j c", j=PACK))
+
+        columns = held("columns", [P, 3 * PACK], F32)
+        bt_rel = held("bt_rel", [P, PACK], F32)
+
+        def turn_vectors():
+            turned = bank("turned")
+            nc.tensor.transpose(turned[:, 0:P], rows[:], identity[:])
+            nc.scalar.copy(columns[:], turned[:, 0 : 3 * PACK])
+            nc.vector.tensor_tensor(bt_rel[:], columns[:, PACK : 2 * PACK], columns[:, 2 * PACK : 3 * PACK], MULT)
+
+        picked = [[held("picked%d%d" % (a, h), [P, PACK, HALF], F32) for h in range(2)] for a in range(PASSES)]
+        x_bf = [[held("x_bf%d%d" % (a, h), [P, HALF, PACK], BF16) for h in range(2)] for a in range(PASSES)]
+        x_codes = [[held("x_codes%d%d" % (a, h), [P, HALF], U32) for h in range(2)] for a in range(PASSES)]
+        x_scales = [[held("x_scales%d%d" % (a, h), [P, HALF], U8) for h in range(2)] for a in range(PASSES)]
+
+        def gather(a, i, h):
+            cols = slice(h * HALF // 16, (h + 1) * HALF // 16)
+            nc.vector.tensor_tensor(picked[a][h][:, i, :], planes[a][i][:].indirect(offsets[:, cols]), weights[h][:], MULT)
+
+        def weave(copy, dst, src):
+            copy(dst.rearrange("p (c i) t -> p c t i", i=4), src.rearrange("p t (c i) -> p c t i", i=4))
+
+        def quantize(codes, scales, src):
+            nc.vector.quantize_mx(out=codes.bitcast(FP8X4), scales=scales, in_=src.rearrange("p n t -> p (n t)"))
+
+        def quantize_x(a, h):
+            quantize(x_codes[a][h][:], x_scales[a][h][:], x_bf[a][h][:])
+
+        ws_codes = held("ws_codes", [P, PASSES * PACK * 2 * P], U8)
+        ws_scale = held("ws_scale", [P, PASSES * PACK * P], U8)
+
+        def deal_ws():
+            nc.vector.tensor_copy(
+                ws_codes[:].bitcast(I32).rearrange("p (a t b w) -> p a t b w", a=PASSES, t=PACK, b=BLOCKS),
+                ws_raw[:].rearrange("p a (b t w) -> p a t b w", b=BLOCKS, t=PACK),
+            )
+            nc.vector.tensor_copy(
+                ws_scale[:].bitcast(I32).rearrange("p (a t b w) -> p a t b w", a=PASSES, t=PACK, b=BLOCKS),
+                ws_scale_raw[:].rearrange("p a (b t w) -> p a t b w", b=BLOCKS, t=PACK),
+            )
+
+        wt_bf = [held("wt_bf%d" % a, [P, H, PACK], BF16) for a in range(PASSES)]
+        wt_codes = [held("wt_codes%d" % a, [P, H], U32) for a in range(PASSES)]
+        wt_scale = [held("wt_scale%d" % a, [P, H], U8) for a in range(PASSES)]
+
+        def cast_wt(a):
+            by_slot = wt_raw[a][:].rearrange("p j (b t e) -> p t j b e", t=PACK, e=RUN)
+            for t in range(PACK):
+                nc.vector.tensor_copy(
+                    wt_bf[a][:, t * P : (t + 1) * P, :].rearrange("p (b u i) j -> p b u j i", b=BLOCKS, i=4),
+                    by_slot[:, t].rearrange("p j b (u i) -> p b u j i", i=4),
+                )
+
+        def quantize_wt(a):
+            quantize(wt_codes[a][:], wt_scale[a][:], wt_bf[a][:])
+
+        def source_pass(acc, a, t, h):
+            u = a * PACK + t
+            nc.tensor.matmul_mx(
+                out=acc[:],
+                lhsT=ws_codes[:, u * 2 * P : (u + 1) * 2 * P].bitcast(FP4X4),
+                lhsT_scale=ws_scale[:, u * P : (u + 1) * P],
+                rhs=x_codes[a][h][:].bitcast(FP8X4),
+                rhs_scale=x_scales[a][h][:],
+                start=(a == 0),
+                stop=(a == PASSES - 1),
+            )
+
+        def target_pass(acc, a, t, h):
+            nc.tensor.matmul_mx(
+                out=acc[:],
+                lhsT=wt_codes[a][:, t * P : (t + 1) * P].bitcast(FP8X4),
+                lhsT_scale=wt_scale[a][:, t * P : (t + 1) * P],
+                rhs=x_codes[a][h][:].bitcast(FP8X4),
+                rhs_scale=x_scales[a][h][:],
+                start=(a == 0),
+                stop=(a == PASSES - 1),
+            )
+
+        h_flat = [[held("h_flat%d%d" % (w, h), [P, PACK, HALF], BF16) for h in range(2)] for w in range(2)]
+        h_bf = [[held("h_bf%d%d" % (w, h), [P, HALF, PACK], BF16) for h in range(2)] for w in range(2)]
+        h_codes = [[held("h_codes%d%d" % (w, h), [P, HALF], U32) for h in range(2)] for w in range(2)]
+        h_scales = [[held("h_scales%d%d" % (w, h), [P, HALF], U8) for h in range(2)] for w in range(2)]
+
+        def empty_source(accs, h):
+            for t in range(PACK):
+                nc.scalar.activation(h_flat[0][h][:, t, :], accs[t][:], IDENTITY, bias=columns[:, t : t + 1])
+
+        def empty_target(accs, h):
+            for t in range(PACK):
+                nc.scalar.activation(
+                    h_flat[1][h][:, t, :], accs[t][:], IDENTITY,
+                    bias=bt_rel[:, t : t + 1], scale=columns[:, 2 * PACK + t : 2 * PACK + t + 1],
+                )
+
+        def weave_h(w, h):
+            weave(nc.vector.tensor_copy, h_bf[w][h][:], h_flat[w][h][:])
+
+        def quantize_h(w, h):
+            quantize(h_codes[w][h][:], h_scales[w][h][:], h_bf[w][h][:])
+
+        def score(hi, m, hj, on_vector):
+            acc = bank("score")
+            nc.tensor.matmul_mx(
+                out=acc[:],
+                lhsT=h_codes[0][hi][:, m * P : (m + 1) * P].bitcast(FP8X4),
+                lhsT_scale=h_scales[0][hi][:, m * P : (m + 1) * P],
+                rhs=h_codes[1][hj][:].bitcast(FP8X4),
+                rhs_scale=h_scales[1][hj][:],
+                start=True,
+                stop=True,
+            )
+            result = stage.tile([P, HALF], F32, name="result")
+            if on_vector:
+                nc.vector.tensor_scalar(result[:], acc[:], 0.0, None, MAX)
+            else:
+                nc.scalar.activation(result[:], acc[:], RELU)
+            r0 = hi * HALF + m * P
+            nc.sync.dma_start(out[r0 : r0 + P, hj * HALF : (hj + 1) * HALF], result[:])
+
+        for i in range(PACK):
+            for h in range(2):
+                gather(0, i, h)
+        for h in range(2):
+            weave(nc.scalar.copy, x_bf[0][h][:], picked[0][h][:])
+        for h in range(2):
+            gather(1, 0, h)
+        deal_ws()
+        for h in range(2):
+            gather(1, 1, h)
+        quantize_x(0, 0)
+        src0 = [bank("src0%d" % t) for t in range(PACK)]
+        for t in range(PACK):
+            source_pass(src0[t], 0, t, 0)
+        for h in range(2):
+            gather(1, 2, h)
+        quantize_x(0, 1)
+        turn_vectors()
+        for h in range(2):
+            gather(1, 3, h)
+            weave(nc.scalar.copy, x_bf[1][h][:], picked[1][h][:])
+        cast_wt(0)
+        quantize_x(1, 0)
+        for t in range(PACK):
+            source_pass(src0[t], 1, t, 0)
+        quantize_wt(0)
+        empty_source(src0, 0)
+        cast_wt(1)
+        quantize_x(1, 1)
+        quantize_wt(1)
+        tgt = [[bank("tgt%d%d" % (h, t)) for t in range(PACK)] for h in range(2)]
+        for t in range(PACK):
+            for a in range(PASSES):
+                target_pass(tgt[0][t], a, t, 0)
+        weave_h(0, 0)
+        empty_target(tgt[0], 0)
+        for t in range(PACK):
+            for a in range(PASSES):
+                target_pass(tgt[1][t], a, t, 1)
+        quantize_h(0, 0)
+        weave_h(1, 0)
+        empty_target(tgt[1], 1)
+        quantize_h(1, 0)
+        for m in range(4):
+            score(0, m, 0, False)
+        src1 = [bank("src1%d" % t) for t in range(PACK)]
+        for t in range(PACK):
+            for a in range(PASSES):
+                source_pass(src1[t], a, t, 1)
+        weave_h(1, 1)
+        quantize_h(1, 1)
+        empty_source(src1, 1)
+        for m in range(4):
+            score(0, m, 1, True)
+        weave_h(0, 1)
+        quantize_h(0, 1)
+        for m in range(4):
+            for hj in range(2):
+                score(1, m, hj, hj == 1)

@@ -4,14 +4,24 @@ import concourse.mybir as mybir
 from concourse.masks import make_identity
 
 K, T, S, H = 1024, 2048, 1024, 512
+FLOPS = 2 * (2 * K * H * S) + 2 * H * S * S
+
 P = 128
-PACK = 4
-K_PASS = P * PACK
+SLOTS = 4
+K_PASS = P * SLOTS
 PASSES = K // K_PASS
 RUN = 8
-BLOCKS = H // (PACK * RUN)
-HALF = S // 2
-FLOPS = 2 * K * H * S * 2 + 2 * H * S * S
+BLOCKS = H // (SLOTS * RUN)
+GROUP = 16
+LINE = 4
+BANKS = 8
+BANK = 512
+TILES = S // P
+HALF = TILES // 2
+QUARTER = TILES // 4
+WOVEN_BUFS = 3
+NARROW_STORES = 10
+WIDE_STORES = 3
 
 F32 = mybir.dt.float32
 BF16 = mybir.dt.bfloat16
@@ -22,243 +32,370 @@ U8 = mybir.dt.uint8
 FP8X4 = mybir.dt.float8_e4m3fn_x4
 FP4X4 = mybir.dt.float4_e2m1fn_x4
 MULT = mybir.AluOpType.mult
+ADD = mybir.AluOpType.add
 MAX = mybir.AluOpType.max
 IDENTITY = mybir.ActivationFunctionType.Identity
 RELU = mybir.ActivationFunctionType.Relu
+
+
+def tiles(lo, hi):
+    return slice(lo * P, hi * P)
+
+
+def quarter(q):
+    return q * QUARTER, (q + 1) * QUARTER
+
+
+def half(h):
+    return h * HALF, (h + 1) * HALF
 
 
 def tile_list_relation_pair_scores_kernel(tc, xT, wgt, offs, ws_words, ws_scales, wt, bs, bt, rel, out):
     nc = tc.nc
     with ExitStack() as ctx:
         keep = ctx.enter_context(tc.tile_pool(name="keep", bufs=1))
-        stage = ctx.enter_context(tc.tile_pool(name="stage", bufs=6))
-        psum = ctx.enter_context(tc.psum_pool(name="psum", bufs=8))
+        ring = ctx.enter_context(tc.tile_pool(name="ring", bufs=WOVEN_BUFS))
+        narrow = ctx.enter_context(tc.tile_pool(name="narrow", bufs=NARROW_STORES))
+        wide = ctx.enter_context(tc.tile_pool(name="wide", bufs=WIDE_STORES))
+        psum = ctx.enter_context(tc.psum_pool(name="psum", bufs=1))
 
         def held(name, shape, dtype):
             return keep.tile(shape, dtype, name=name, align_bytes=64)
 
-        def bank(name):
-            return psum.tile([P, HALF], F32, name=name, tag="bank")
+        free_banks = list(range(BANKS))
+        taken = {}
 
-        offsets = keep.tile([P, S // 16], U16, name="offsets")
-        nc.sync.dma_start(offsets[:], offs)
-        planes = [[held("plane%d%d" % (a, i), [P, T], F32) for i in range(PACK)] for a in range(PASSES)]
-        weights = [held("weights%d" % h, [P, HALF], F32) for h in range(2)]
+        def take_bank(user):
+            number = free_banks.pop(0)
+            acc = psum.tile([P, BANK], F32, name="bank%d" % number, tag="bank%d" % number)
+            taken[user] = (number, acc)
+            return acc
+
+        def bank_of(user):
+            return taken[user][1]
+
+        def give_bank(user):
+            free_banks.append(taken.pop(user)[0])
+
+        offsets = keep.tile([P, S // GROUP], U16, name="offsets")
+        planes = [[held("plane%d%d" % (a, t), [P, T], F32) for t in range(SLOTS)] for a in range(PASSES)]
+        weights = held("weights", [P, S], F32)
         ws_raw = held("ws_raw", [P, PASSES, 2 * H // 4], I32)
-        wt_raw = [held("wt_raw%d" % a, [P, PACK, H], F32) for a in range(PASSES)]
-
-        def load_plane(a, i):
-            nc.sync.dma_start(planes[a][i][:], xT[a * K_PASS + i : (a + 1) * K_PASS : PACK, :])
-
         ws_scale_raw = held("ws_scale_raw", [P, PASSES, H // 4], I32)
-        nc.vector.memset(ws_scale_raw[:], 0)
-        rows = held("rows", [P, P], F32)
-        nc.vector.memset(rows[:], 0.0)
+        wt_raw = [held("wt_raw%d" % a, [P, SLOTS, H], F32) for a in range(PASSES)]
+        vector_rows = held("vector_rows", [P, P], F32)
         identity = held("identity", [P, P], F32)
+        nc.vector.memset(ws_scale_raw[:], 0)
+        nc.vector.memset(vector_rows[:], 0.0)
         make_identity(nc, identity[:])
 
-        def load_scales(q):
+        def load_plane(a, t):
+            nc.sync.dma_start(planes[a][t][:], xT[a * K_PASS + t : (a + 1) * K_PASS : SLOTS, :])
+
+        def load_weights(h):
+            nc.sync.dma_start(weights[:, tiles(*half(h))], wgt[:, tiles(*half(h))])
+
+        def load_ws_scales(quadrant):
             nc.sync.dma_start(
-                ws_scale_raw[32 * q : 32 * q + 4, :, :],
-                ws_scales[:, 4 * q : 4 * q + 4, :].rearrange("a q c -> q a c").bitcast(I32),
+                ws_scale_raw[32 * quadrant : 32 * quadrant + 4, :, :],
+                ws_scales[:, 4 * quadrant : 4 * quadrant + 4, :].rearrange("a q c -> q a c").bitcast(I32),
             )
 
-        def load_vector(v, vec):
+        def load_vector(v, vector):
             nc.sync.dma_start(
-                rows[PACK * v : PACK * (v + 1), :].rearrange("t (b e) -> t b e", e=RUN),
-                vec.rearrange("(b t e) -> t b e", t=PACK, e=RUN),
+                vector_rows[SLOTS * v : SLOTS * (v + 1), :].rearrange("t (b e) -> t b e", e=RUN),
+                vector.rearrange("(b t e) -> t b e", t=SLOTS, e=RUN),
             )
+
+        def load_wt(a, b0, b1):
+            cols = slice(b0 * SLOTS * RUN, b1 * SLOTS * RUN)
+            rows = wt[a * K_PASS : (a + 1) * K_PASS, :].rearrange("(p j) c -> p j c", j=SLOTS)
+            nc.sync.dma_start(wt_raw[a][:, :, cols], rows[:, :, cols])
 
         load_plane(0, 0)
-        for h in range(2):
-            nc.sync.dma_start(weights[h][:], wgt[:, h * HALF : (h + 1) * HALF])
-        for i in range(1, PACK):
-            load_plane(0, i)
-            load_scales(i - 1)
-        load_scales(3)
+        load_weights(0)
+        nc.sync.dma_start(offsets[:], offs)
+        load_weights(1)
+        for t in range(1, SLOTS):
+            load_plane(0, t)
+            load_ws_scales(t - 1)
+        load_ws_scales(SLOTS - 1)
+        load_plane(1, 0)
+        load_vector(0, bs)
+        load_plane(1, 1)
+        load_vector(1, bt)
+        load_wt(1, 0, BLOCKS)
+        load_vector(2, rel)
+        load_wt(0, 0, BLOCKS // 2)
+        load_plane(1, 2)
         nc.sync.dma_start(ws_raw[:], ws_words.rearrange("a p c -> p a c").bitcast(I32))
-        for i, vec in enumerate((bs, bt, rel)):
-            load_plane(1, i)
-            load_vector(i, vec)
+        load_wt(0, BLOCKS // 2, BLOCKS)
         load_plane(1, 3)
-        for a in range(PASSES):
-            nc.sync.dma_start(wt_raw[a][:], wt[a * K_PASS : (a + 1) * K_PASS, :].rearrange("(p j) c -> p j c", j=PACK))
 
-        columns = held("columns", [P, 3 * PACK], F32)
-        bt_rel = held("bt_rel", [P, PACK], F32)
-
-        def turn_vectors():
-            turned = bank("turned")
-            nc.tensor.transpose(turned[:, 0:P], rows[:], identity[:])
-            nc.scalar.copy(columns[:], turned[:, 0 : 3 * PACK])
-            nc.vector.tensor_tensor(bt_rel[:], columns[:, PACK : 2 * PACK], columns[:, 2 * PACK : 3 * PACK], MULT)
-
-        picked = [[held("picked%d%d" % (a, h), [P, PACK, HALF], F32) for h in range(2)] for a in range(PASSES)]
-        x_bf = [[held("x_bf%d%d" % (a, h), [P, HALF, PACK], BF16) for h in range(2)] for a in range(PASSES)]
-        x_codes = [[held("x_codes%d%d" % (a, h), [P, HALF], U32) for h in range(2)] for a in range(PASSES)]
-        x_scales = [[held("x_scales%d%d" % (a, h), [P, HALF], U8) for h in range(2)] for a in range(PASSES)]
-
-        def gather(a, i, h):
-            cols = slice(h * HALF // 16, (h + 1) * HALF // 16)
-            nc.vector.tensor_tensor(picked[a][h][:, i, :], planes[a][i][:].indirect(offsets[:, cols]), weights[h][:], MULT)
-
-        def weave(copy, dst, src):
-            copy(dst.rearrange("p (c i) t -> p c t i", i=4), src.rearrange("p t (c i) -> p c t i", i=4))
+        def interleave(copy, dst, src):
+            copy(dst.rearrange("p (c i) t -> p c t i", i=LINE), src.rearrange("p t (c i) -> p c t i", i=LINE))
 
         def quantize(codes, scales, src):
             nc.vector.quantize_mx(out=codes.bitcast(FP8X4), scales=scales, in_=src.rearrange("p n t -> p (n t)"))
 
-        def quantize_x(a, h):
-            quantize(x_codes[a][h][:], x_scales[a][h][:], x_bf[a][h][:])
+        columns = held("columns", [P, 3 * SLOTS], F32)
+        bs_cols, bt_cols, rel_cols = (columns[:, v * SLOTS : (v + 1) * SLOTS] for v in range(3))
+        bt_rel = held("bt_rel", [P, SLOTS], F32)
 
-        ws_codes = held("ws_codes", [P, PASSES * PACK * 2 * P], U8)
-        ws_scale = held("ws_scale", [P, PASSES * PACK * P], U8)
+        def turn_vectors():
+            turned = take_bank("turn")
+            nc.tensor.transpose(turned[:, 0:P], vector_rows[:], identity[:])
+            nc.scalar.copy(columns[:], turned[:, 0 : 3 * SLOTS])
+            give_bank("turn")
+            nc.vector.tensor_tensor(bt_rel[:], bt_cols, rel_cols, MULT)
 
-        def deal_ws():
-            nc.vector.tensor_copy(
-                ws_codes[:].bitcast(I32).rearrange("p (a t b w) -> p a t b w", a=PASSES, t=PACK, b=BLOCKS),
-                ws_raw[:].rearrange("p a (b t w) -> p a t b w", b=BLOCKS, t=PACK),
+        picked = [held("picked%d" % a, [P, SLOTS, S], F32) for a in range(PASSES)]
+        x_codes = [held("x_codes%d" % a, [P, S], U32) for a in range(PASSES)]
+        x_scales = [held("x_scales%d" % a, [P, S], U8) for a in range(PASSES)]
+        x_woven = held("x_woven", [P, S, SLOTS], BF16)
+        x_woven_last = {}
+
+        def gather(a, t, lo, hi):
+            listed = offsets[:, lo * P // GROUP : hi * P // GROUP]
+            nc.vector.tensor_tensor(
+                picked[a][:, t, tiles(lo, hi)], planes[a][t][:].indirect(listed), weights[:, tiles(lo, hi)], MULT
             )
-            nc.vector.tensor_copy(
-                ws_scale[:].bitcast(I32).rearrange("p (a t b w) -> p a t b w", a=PASSES, t=PACK, b=BLOCKS),
-                ws_scale_raw[:].rearrange("p a (b t w) -> p a t b w", b=BLOCKS, t=PACK),
-            )
 
-        wt_bf = [held("wt_bf%d" % a, [P, H, PACK], BF16) for a in range(PASSES)]
-        wt_codes = [held("wt_codes%d" % a, [P, H], U32) for a in range(PASSES)]
-        wt_scale = [held("wt_scale%d" % a, [P, H], U8) for a in range(PASSES)]
+        def quantize_x(h):
+            cols = tiles(*half(h))
+            quantize(x_codes[0][:, cols], x_scales[0][:, cols], x_woven[:, cols, :])
 
-        def cast_wt(a):
-            by_slot = wt_raw[a][:].rearrange("p j (b t e) -> p t j b e", t=PACK, e=RUN)
-            for t in range(PACK):
+        def interleave_x_last(copy, q):
+            x_woven_last[q] = ring.tile([P, QUARTER * P, SLOTS], BF16, name="x_woven_last", align_bytes=64)
+            interleave(copy, x_woven_last[q][:], picked[1][:, :, tiles(*quarter(q))])
+
+        def quantize_x_last(q):
+            cols = tiles(*quarter(q))
+            quantize(x_codes[1][:, cols], x_scales[1][:, cols], x_woven_last[q][:])
+
+        ws_codes = held("ws_codes", [P, PASSES * H * 2], U8)
+        ws_scale = held("ws_scale", [P, PASSES * H], U8)
+
+        def order_ws():
+            for dst, src in ((ws_codes, ws_raw), (ws_scale, ws_scale_raw)):
                 nc.vector.tensor_copy(
-                    wt_bf[a][:, t * P : (t + 1) * P, :].rearrange("p (b u i) j -> p b u j i", b=BLOCKS, i=4),
-                    by_slot[:, t].rearrange("p j b (u i) -> p b u j i", i=4),
+                    dst[:].bitcast(I32).rearrange("p (a t b w) -> p a t b w", a=PASSES, t=SLOTS, b=BLOCKS),
+                    src[:].rearrange("p a (b t w) -> p a t b w", b=BLOCKS, t=SLOTS),
+                )
+
+        wt_woven = held("wt_woven", [P, PASSES * H, SLOTS], BF16)
+        wt_codes = held("wt_codes", [P, PASSES * H], U32)
+        wt_scale = held("wt_scale", [P, PASSES * H], U8)
+
+        def cast_wt(a, b0, b1):
+            by_slot = wt_raw[a][:].rearrange("p j (b t e) -> p t j b e", t=SLOTS, e=RUN)
+            for t in range(SLOTS):
+                first = a * H + t * P
+                nc.scalar.copy(
+                    wt_woven[:, first + b0 * RUN : first + b1 * RUN, :].rearrange(
+                        "p (b u i) j -> p b u j i", u=RUN // LINE, i=LINE
+                    ),
+                    by_slot[:, t, :, b0:b1, :].rearrange("p j b (u i) -> p b u j i", i=LINE),
                 )
 
         def quantize_wt(a):
-            quantize(wt_codes[a][:], wt_scale[a][:], wt_bf[a][:])
+            cols = slice(a * H, (a + 1) * H)
+            quantize(wt_codes[:, cols], wt_scale[:, cols], wt_woven[:, cols, :])
 
-        def source_pass(acc, a, t, h):
-            u = a * PACK + t
-            nc.tensor.matmul_mx(
-                out=acc[:],
-                lhsT=ws_codes[:, u * 2 * P : (u + 1) * 2 * P].bitcast(FP4X4),
-                lhsT_scale=ws_scale[:, u * P : (u + 1) * P],
-                rhs=x_codes[a][h][:].bitcast(FP8X4),
-                rhs_scale=x_scales[a][h][:],
-                start=(a == 0),
-                stop=(a == PASSES - 1),
-            )
-
-        def target_pass(acc, a, t, h):
-            nc.tensor.matmul_mx(
-                out=acc[:],
-                lhsT=wt_codes[a][:, t * P : (t + 1) * P].bitcast(FP8X4),
-                lhsT_scale=wt_scale[a][:, t * P : (t + 1) * P],
-                rhs=x_codes[a][h][:].bitcast(FP8X4),
-                rhs_scale=x_scales[a][h][:],
-                start=(a == 0),
-                stop=(a == PASSES - 1),
-            )
-
-        h_flat = [[held("h_flat%d%d" % (w, h), [P, PACK, HALF], BF16) for h in range(2)] for w in range(2)]
-        h_bf = [[held("h_bf%d%d" % (w, h), [P, HALF, PACK], BF16) for h in range(2)] for w in range(2)]
-        h_codes = [[held("h_codes%d%d" % (w, h), [P, HALF], U32) for h in range(2)] for w in range(2)]
-        h_scales = [[held("h_scales%d%d" % (w, h), [P, HALF], U8) for h in range(2)] for w in range(2)]
-
-        def empty_source(accs, h):
-            for t in range(PACK):
-                nc.scalar.activation(h_flat[0][h][:, t, :], accs[t][:], IDENTITY, bias=columns[:, t : t + 1])
-
-        def empty_target(accs, h):
-            for t in range(PACK):
-                nc.scalar.activation(
-                    h_flat[1][h][:, t, :], accs[t][:], IDENTITY,
-                    bias=bt_rel[:, t : t + 1], scale=columns[:, 2 * PACK + t : 2 * PACK + t + 1],
+        def source_pass(a, m):
+            if a == 0:
+                take_bank(("source", m))
+            for t in range(SLOTS):
+                u = a * SLOTS + t
+                nc.tensor.matmul_mx(
+                    out=bank_of(("source", m))[:, tiles(t, t + 1)],
+                    lhsT=ws_codes[:, tiles(2 * u, 2 * u + 2)].bitcast(FP4X4),
+                    lhsT_scale=ws_scale[:, tiles(u, u + 1)],
+                    rhs=x_codes[a][:, tiles(m, m + 1)].bitcast(FP8X4),
+                    rhs_scale=x_scales[a][:, tiles(m, m + 1)],
+                    start=(a == 0 and t == 0),
+                    stop=(a == PASSES - 1 and t == SLOTS - 1),
                 )
 
-        def weave_h(w, h):
-            weave(nc.vector.tensor_copy, h_bf[w][h][:], h_flat[w][h][:])
+        def target_sums(q, t):
+            return bank_of(("target", q, t // 2))[:, tiles(*quarter(t % 2))]
 
-        def quantize_h(w, h):
-            quantize(h_codes[w][h][:], h_scales[w][h][:], h_bf[w][h][:])
+        def target_pass(a, q):
+            for t in range(SLOTS):
+                if a == 0 and t % 2 == 0:
+                    take_bank(("target", q, t // 2))
+                u = a * SLOTS + t
+                nc.tensor.matmul_mx(
+                    out=target_sums(q, t),
+                    lhsT=wt_codes[:, tiles(u, u + 1)].bitcast(FP8X4),
+                    lhsT_scale=wt_scale[:, tiles(u, u + 1)],
+                    rhs=x_codes[a][:, tiles(*quarter(q))].bitcast(FP8X4),
+                    rhs_scale=x_scales[a][:, tiles(*quarter(q))],
+                    start=(a == 0 and t % 2 == 0),
+                    stop=(a == PASSES - 1 and t % 2 == 1),
+                )
 
-        def score(hi, m, hj, on_vector):
-            acc = bank("score")
-            nc.tensor.matmul_mx(
-                out=acc[:],
-                lhsT=h_codes[0][hi][:, m * P : (m + 1) * P].bitcast(FP8X4),
-                lhsT_scale=h_scales[0][hi][:, m * P : (m + 1) * P],
-                rhs=h_codes[1][hj][:].bitcast(FP8X4),
-                rhs_scale=h_scales[1][hj][:],
-                start=True,
-                stop=True,
+        hs_woven = held("hs_woven", [P, S, SLOTS], BF16)
+        hs_codes = held("hs_codes", [P, S], U32)
+        hs_scales = held("hs_scales", [P, S], U8)
+        ht_flat = held("ht_flat", [P, SLOTS, S], BF16)
+        ht_woven = held("ht_woven", [P, S, SLOTS], BF16)
+        ht_codes = held("ht_codes", [P, S], U32)
+        ht_scales = held("ht_scales", [P, S], U8)
+
+        def empty_source(m):
+            nc.vector.tensor_tensor(
+                hs_woven[:, tiles(m, m + 1), :],
+                bank_of(("source", m))[:].rearrange("p (t n) -> p n t", t=SLOTS),
+                bs_cols.unsqueeze(1).to_broadcast([P, P, SLOTS]),
+                ADD,
             )
-            result = stage.tile([P, HALF], F32, name="result")
-            if on_vector:
-                nc.vector.tensor_scalar(result[:], acc[:], 0.0, None, MAX)
-            else:
-                nc.scalar.activation(result[:], acc[:], RELU)
-            r0 = hi * HALF + m * P
-            nc.sync.dma_start(out[r0 : r0 + P, hj * HALF : (hj + 1) * HALF], result[:])
+            give_bank(("source", m))
 
-        for i in range(PACK):
+        def quantize_source(lo, hi):
+            quantize(hs_codes[:, tiles(lo, hi)], hs_scales[:, tiles(lo, hi)], hs_woven[:, tiles(lo, hi), :])
+
+        def empty_target(q):
+            for t in range(SLOTS):
+                nc.scalar.activation(
+                    ht_flat[:, t, tiles(*quarter(q))],
+                    target_sums(q, t),
+                    IDENTITY,
+                    bias=bt_rel[:, t : t + 1],
+                    scale=rel_cols[:, t : t + 1],
+                )
+            for pair in range(2):
+                give_bank(("target", q, pair))
+
+        def interleave_target(q):
+            cols = tiles(*quarter(q))
+            interleave(nc.vector.tensor_copy, ht_woven[:, cols, :], ht_flat[:, :, cols])
+
+        def quantize_target(q):
+            cols = tiles(*quarter(q))
+            quantize(ht_codes[:, cols], ht_scales[:, cols], ht_woven[:, cols, :])
+
+        def relu_on_scalar(dst, acc):
+            nc.scalar.activation(dst, acc, RELU)
+
+        def relu_on_vector(dst, acc):
+            nc.vector.tensor_scalar(dst, acc, 0.0, None, MAX)
+
+        def score_bank(user, sources, targets, relu, dst):
+            acc = take_bank(user)
+            width = targets[1] - targets[0]
+            for u, m in enumerate(range(*sources)):
+                nc.tensor.matmul_mx(
+                    out=acc[:, tiles(u * width, (u + 1) * width)],
+                    lhsT=hs_codes[:, tiles(m, m + 1)].bitcast(FP8X4),
+                    lhsT_scale=hs_scales[:, tiles(m, m + 1)],
+                    rhs=ht_codes[:, tiles(*targets)].bitcast(FP8X4),
+                    rhs_scale=ht_scales[:, tiles(*targets)],
+                    start=True,
+                    stop=True,
+                )
+            relu(dst, acc[:])
+
+        def score_block(sources, targets):
+            result = narrow.tile([P, BANK], F32, name="result")
+            score_bank("block", sources, targets, relu_on_scalar, result[:])
+            give_bank("block")
+            nc.sync.dma_start(
+                out[tiles(*sources), tiles(*targets)].rearrange("(u p) j -> p u j", p=P),
+                result[:].rearrange("p (u j) -> p u j", u=sources[1] - sources[0]),
+            )
+
+        def score_row(m, relus):
+            row = wide.tile([P, S], F32, name="row")
             for h in range(2):
-                gather(0, i, h)
+                score_bank(("row", h), (m, m + 1), half(h), relus[h], row[:, tiles(*half(h))])
+            for h in range(2):
+                give_bank(("row", h))
+            nc.sync.dma_start(out[tiles(m, m + 1), :], row[:])
+
+        for t in range(SLOTS):
+            if t in (0, SLOTS - 1):
+                for h in range(2):
+                    gather(0, t, *half(h))
+            else:
+                gather(0, t, 0, TILES)
         for h in range(2):
-            weave(nc.scalar.copy, x_bf[0][h][:], picked[0][h][:])
-        for h in range(2):
-            gather(1, 0, h)
-        deal_ws()
-        for h in range(2):
-            gather(1, 1, h)
-        quantize_x(0, 0)
-        src0 = [bank("src0%d" % t) for t in range(PACK)]
-        for t in range(PACK):
-            source_pass(src0[t], 0, t, 0)
-        for h in range(2):
-            gather(1, 2, h)
-        quantize_x(0, 1)
+            cols = tiles(*half(h))
+            interleave(nc.scalar.copy, x_woven[:, cols, :], picked[0][:, :, cols])
+        gather(1, 0, 0, TILES)
+        quantize_x(0)
+        cast_wt(1, 0, BLOCKS)
         turn_vectors()
-        for h in range(2):
-            gather(1, 3, h)
-            weave(nc.scalar.copy, x_bf[1][h][:], picked[1][h][:])
-        cast_wt(0)
-        quantize_x(1, 0)
-        for t in range(PACK):
-            source_pass(src0[t], 1, t, 0)
-        quantize_wt(0)
-        empty_source(src0, 0)
-        cast_wt(1)
-        quantize_x(1, 1)
+        gather(1, 1, 0, TILES)
+        quantize_x(1)
         quantize_wt(1)
-        tgt = [[bank("tgt%d%d" % (h, t)) for t in range(PACK)] for h in range(2)]
-        for t in range(PACK):
-            for a in range(PASSES):
-                target_pass(tgt[0][t], a, t, 0)
-        weave_h(0, 0)
-        empty_target(tgt[0], 0)
-        for t in range(PACK):
-            for a in range(PASSES):
-                target_pass(tgt[1][t], a, t, 1)
-        quantize_h(0, 0)
-        weave_h(1, 0)
-        empty_target(tgt[1], 1)
-        quantize_h(1, 0)
-        for m in range(4):
-            score(0, m, 0, False)
-        src1 = [bank("src1%d" % t) for t in range(PACK)]
-        for t in range(PACK):
-            for a in range(PASSES):
-                source_pass(src1[t], a, t, 1)
-        weave_h(1, 1)
-        quantize_h(1, 1)
-        empty_source(src1, 1)
-        for m in range(4):
-            score(0, m, 1, True)
-        weave_h(0, 1)
-        quantize_h(0, 1)
-        for m in range(4):
-            for hj in range(2):
-                score(1, m, hj, hj == 1)
+        cast_wt(0, 0, BLOCKS // 2)
+        gather(1, 2, 0, TILES)
+        order_ws()
+        cast_wt(0, BLOCKS // 2, BLOCKS)
+        quantize_wt(0)
+
+        for m in range(HALF):
+            source_pass(0, m)
+        for q in range(2):
+            target_pass(0, q)
+
+        for q in range(4):
+            gather(1, SLOTS - 1, *quarter(q))
+        for q in range(2):
+            interleave_x_last(nc.scalar.copy, q)
+        for q in range(2):
+            quantize_x_last(q)
+            target_pass(1, q)
+            for m in range(*quarter(q)):
+                source_pass(1, m)
+            if q == 0:
+                interleave_x_last(nc.scalar.copy, 2)
+            empty_target(q)
+        interleave_x_last(nc.vector.tensor_copy, 3)
+        quantize_x_last(2)
+        for a in range(PASSES):
+            target_pass(a, 2)
+
+        for m in range(*quarter(0)):
+            empty_source(m)
+        interleave_target(0)
+        quantize_source(*quarter(0))
+        quantize_target(0)
+        quantize_x_last(3)
+        for a in range(PASSES):
+            target_pass(a, 3)
+        score_block(quarter(0), quarter(0))
+        interleave_target(1)
+        quantize_target(1)
+        score_block(quarter(0), quarter(1))
+        empty_target(2)
+        for m in range(*quarter(1)):
+            empty_source(m)
+            quantize_source(m, m + 1)
+            score_block((m, m + 1), half(0))
+        empty_target(3)
+        for q in (2, 3):
+            if q == 2:
+                for m in range(*quarter(q)):
+                    for a in range(PASSES):
+                        source_pass(a, m)
+            interleave_target(q)
+            quantize_target(q)
+            for source_q in range(2):
+                score_block(quarter(source_q), quarter(q))
+            if q == 2:
+                for m in range(*quarter(3)):
+                    for a in range(PASSES):
+                        source_pass(a, m)
+        empty_source(HALF)
+        quantize_source(HALF, HALF + 1)
+        for h in range(2):
+            score_block((HALF, HALF + 1), half(h))
+        last_rows = range(HALF + 1, TILES)
+        for m in last_rows:
+            empty_source(m)
+            quantize_source(m, m + 1)
+        last_relus = ((relu_on_scalar, relu_on_scalar), (relu_on_vector, relu_on_vector), (relu_on_scalar, relu_on_vector))
+        for m, relus in zip(last_rows, last_relus):
+            score_row(m, relus)

@@ -83,7 +83,7 @@ def tile_list_relation_pair_scores_kernel(tc, xT, wgt, offs, ws_words, ws_scales
         ws_raw = held("ws_raw", [P, PASSES, 2 * H // 4], I32)
         ws_scale_raw = held("ws_scale_raw", [P, PASSES, H // 4], I32)
         wt_raw = [held("wt_raw%d" % a, [P, SLOTS, H], F32) for a in range(PASSES)]
-        vector_rows = held("vector_rows", [P, P], F32)
+        vector_rows = held("vector_rows", [P, H], F32)
         identity = held("identity", [P, P], F32)
         nc.vector.memset(ws_scale_raw[:], 0)
         nc.vector.memset(vector_rows[:], 0.0)
@@ -102,10 +102,7 @@ def tile_list_relation_pair_scores_kernel(tc, xT, wgt, offs, ws_words, ws_scales
             )
 
         def load_vector(v, vector):
-            nc.sync.dma_start(
-                vector_rows[SLOTS * v : SLOTS * (v + 1), :].rearrange("t (b e) -> t b e", e=RUN),
-                vector.rearrange("(b t e) -> t b e", t=SLOTS, e=RUN),
-            )
+            nc.sync.dma_start(vector_rows[v : v + 1, :], vector.unsqueeze(0))
 
         def load_wt(a, b0, b1):
             cols = slice(b0 * SLOTS * RUN, b1 * SLOTS * RUN)
@@ -116,17 +113,16 @@ def tile_list_relation_pair_scores_kernel(tc, xT, wgt, offs, ws_words, ws_scales
         load_weights(0)
         nc.sync.dma_start(offsets[:], offs)
         load_weights(1)
-        for t in range(1, SLOTS):
-            load_plane(0, t)
-            load_ws_scales(t - 1)
-        load_ws_scales(SLOTS - 1)
-        load_plane(1, 0)
-        load_vector(0, bs)
-        load_plane(1, 1)
-        load_vector(1, bt)
+        for v, vector in enumerate((bs, bt, rel)):
+            load_vector(v, vector)
+            load_plane(0, v + 1)
+        for t in range(2):
+            load_plane(1, t)
+            load_ws_scales(t)
         load_wt(1, 0, BLOCKS)
-        load_vector(2, rel)
+        load_ws_scales(2)
         load_wt(0, 0, BLOCKS // 2)
+        load_ws_scales(3)
         load_plane(1, 2)
         nc.sync.dma_start(ws_raw[:], ws_words.rearrange("a p c -> p a c").bitcast(I32))
         load_wt(0, BLOCKS // 2, BLOCKS)
@@ -143,11 +139,21 @@ def tile_list_relation_pair_scores_kernel(tc, xT, wgt, offs, ws_words, ws_scales
         bt_rel = held("bt_rel", [P, SLOTS], F32)
 
         def turn_vectors():
+            by_slot = held("vector_rows_by_slot", [P, H], F32)
+            nc.scalar.copy(
+                by_slot[:].rearrange("v (t b e) -> v t b e", t=SLOTS, e=RUN),
+                vector_rows[:].rearrange("v (b t e) -> v t b e", t=SLOTS, e=RUN),
+            )
             turned = take_bank("turn")
-            nc.tensor.transpose(turned[:, 0:P], vector_rows[:], identity[:])
-            nc.scalar.copy(columns[:], turned[:, 0 : 3 * SLOTS])
+            for t in range(SLOTS):
+                nc.tensor.transpose(turned[:, tiles(t, t + 1)], by_slot[:, tiles(t, t + 1)], identity[:])
+            nc.scalar.copy(
+                columns[:].rearrange("p (v t) -> p v t", t=SLOTS),
+                turned[:].rearrange("p (t v) -> p v t", t=SLOTS)[:, 0:3, :],
+            )
             give_bank("turn")
-            nc.vector.tensor_tensor(bt_rel[:], bt_cols, rel_cols, MULT)
+            for t in range(SLOTS):
+                nc.scalar.activation(bt_rel[:, t : t + 1], bt_cols[:, t : t + 1], IDENTITY, scale=rel_cols[:, t : t + 1])
 
         picked = [held("picked%d" % a, [P, SLOTS, S], F32) for a in range(PASSES)]
         x_codes = [held("x_codes%d" % a, [P, S], U32) for a in range(PASSES)]
@@ -319,13 +325,13 @@ def tile_list_relation_pair_scores_kernel(tc, xT, wgt, offs, ws_words, ws_scales
                     gather(0, t, *half(h))
             else:
                 gather(0, t, 0, TILES)
+        turn_vectors()
         for h in range(2):
             cols = tiles(*half(h))
             interleave(nc.scalar.copy, x_woven[:, cols, :], picked[0][:, :, cols])
         gather(1, 0, 0, TILES)
         quantize_x(0)
         cast_wt(1, 0, BLOCKS)
-        turn_vectors()
         gather(1, 1, 0, TILES)
         quantize_x(1)
         quantize_wt(1)
@@ -362,10 +368,10 @@ def tile_list_relation_pair_scores_kernel(tc, xT, wgt, offs, ws_words, ws_scales
         interleave_target(0)
         quantize_source(*quarter(0))
         quantize_target(0)
+        score_block(quarter(0), quarter(0))
         quantize_x_last(3)
         for a in range(PASSES):
             target_pass(a, 3)
-        score_block(quarter(0), quarter(0))
         interleave_target(1)
         quantize_target(1)
         score_block(quarter(0), quarter(1))

from contextlib import ExitStack

import concourse.mybir as mybir
from concourse.masks import make_identity

K, T, S, H = 1024, 2048, 1024, 512
FLOPS = 2 * (2 * K * H * S) + 2 * H * S * S

P = 128
SLOTS = 4
K_PASS = P * SLOTS
PASSES = K // K_PASS
RUN = 8
BLOCKS = H // (SLOTS * RUN)
GROUP = 16
LINE = 4
BANKS = 8
BANK = 512
TILES = S // P
HALF = TILES // 2
QUARTER = TILES // 4
WOVEN_BUFS = 3
NARROW_STORES = 10
WIDE_STORES = 3

F32 = mybir.dt.float32
BF16 = mybir.dt.bfloat16
I32 = mybir.dt.int32
U32 = mybir.dt.uint32
U16 = mybir.dt.uint16
U8 = mybir.dt.uint8
FP8X4 = mybir.dt.float8_e4m3fn_x4
FP4X4 = mybir.dt.float4_e2m1fn_x4
MULT = mybir.AluOpType.mult
ADD = mybir.AluOpType.add
MAX = mybir.AluOpType.max
IDENTITY = mybir.ActivationFunctionType.Identity
RELU = mybir.ActivationFunctionType.Relu


def tiles(lo, hi):
    return slice(lo * P, hi * P)


def quarter(q):
    return q * QUARTER, (q + 1) * QUARTER


def half(h):
    return h * HALF, (h + 1) * HALF


def tile_list_relation_pair_scores_kernel(tc, xT, wgt, offs, ws_words, ws_scales, wt, bs, bt, rel, out):
    nc = tc.nc
    with ExitStack() as ctx:
        keep = ctx.enter_context(tc.tile_pool(name="keep", bufs=1))
        ring = ctx.enter_context(tc.tile_pool(name="ring", bufs=WOVEN_BUFS))
        narrow = ctx.enter_context(tc.tile_pool(name="narrow", bufs=NARROW_STORES))
        wide = ctx.enter_context(tc.tile_pool(name="wide", bufs=WIDE_STORES))
        psum = ctx.enter_context(tc.psum_pool(name="psum", bufs=1))

        def held(name, shape, dtype):
            return keep.tile(shape, dtype, name=name, align_bytes=64)

        free_banks = list(range(BANKS))
        taken = {}

        def take_bank(user):
            number = free_banks.pop(0)
            acc = psum.tile([P, BANK], F32, name="bank%d" % number, tag="bank%d" % number)
            taken[user] = (number, acc)
            return acc

        def bank_of(user):
            return taken[user][1]

        def give_bank(user):
            free_banks.append(taken.pop(user)[0])

        offsets = keep.tile([P, S // GROUP], U16, name="offsets")
        planes = [[held("plane%d%d" % (a, t), [P, T], F32) for t in range(SLOTS)] for a in range(PASSES)]
        weights = held("weights", [P, S], F32)
        ws_raw = held("ws_raw", [P, PASSES, 2 * H // 4], I32)
        ws_scale_raw = held("ws_scale_raw", [P, PASSES, H // 4], I32)
        wt_raw = [held("wt_raw%d" % a, [P, SLOTS, H], F32) for a in range(PASSES)]
        vector_rows = held("vector_rows", [P, H], F32)
        identity = held("identity", [P, P], F32)
        nc.vector.memset(ws_scale_raw[:], 0)
        nc.vector.memset(vector_rows[:], 0.0)
        make_identity(nc, identity[:])

        def load_plane(a, t):
            nc.sync.dma_start(planes[a][t][:], xT[a * K_PASS + t : (a + 1) * K_PASS : SLOTS, :])

        def load_weights(h):
            nc.sync.dma_start(weights[:, tiles(*half(h))], wgt[:, tiles(*half(h))])

        def load_ws_scales(quadrant):
            nc.sync.dma_start(
                ws_scale_raw[32 * quadrant : 32 * quadrant + 4, :, :],
                ws_scales[:, 4 * quadrant : 4 * quadrant + 4, :].rearrange("a q c -> q a c").bitcast(I32),
            )

        def load_vector(v, vector):
            nc.sync.dma_start(vector_rows[v : v + 1, :], vector.unsqueeze(0))

        def load_wt(a, b0, b1):
            cols = slice(b0 * SLOTS * RUN, b1 * SLOTS * RUN)
            rows = wt[a * K_PASS : (a + 1) * K_PASS, :].rearrange("(p j) c -> p j c", j=SLOTS)
            nc.sync.dma_start(wt_raw[a][:, :, cols], rows[:, :, cols])

        load_plane(0, 0)
        load_weights(0)
        nc.sync.dma_start(offsets[:], offs)
        load_weights(1)
        for v, vector in enumerate((bs, bt, rel)):
            load_vector(v, vector)
            load_plane(0, v + 1)
        for t in range(2):
            load_plane(1, t)
            load_ws_scales(t)
        load_wt(1, 0, BLOCKS)
        load_ws_scales(2)
        load_wt(0, 0, BLOCKS // 2)
        load_ws_scales(3)
        load_plane(1, 2)
        nc.sync.dma_start(ws_raw[:], ws_words.rearrange("a p c -> p a c").bitcast(I32))
        load_wt(0, BLOCKS // 2, BLOCKS)
        load_plane(1, 3)

        def interleave(copy, dst, src):
            copy(dst.rearrange("p (c i) t -> p c t i", i=LINE), src.rearrange("p t (c i) -> p c t i", i=LINE))

        def quantize(codes, scales, src):
            nc.vector.quantize_mx(out=codes.bitcast(FP8X4), scales=scales, in_=src.rearrange("p n t -> p (n t)"))

        columns = held("columns", [P, 3 * SLOTS], F32)
        bs_cols, bt_cols, rel_cols = (columns[:, v * SLOTS : (v + 1) * SLOTS] for v in range(3))
        bt_rel = held("bt_rel", [P, SLOTS], F32)

        def turn_vectors():
            by_slot = held("vector_rows_by_slot", [P, H], F32)
            nc.scalar.copy(
                by_slot[:].rearrange("v (t b e) -> v t b e", t=SLOTS, e=RUN),
                vector_rows[:].rearrange("v (b t e) -> v t b e", t=SLOTS, e=RUN),
            )
            turned = take_bank("turn")
            for t in range(SLOTS):
                nc.tensor.transpose(turned[:, tiles(t, t + 1)], by_slot[:, tiles(t, t + 1)], identity[:])
            nc.scalar.copy(
                columns[:].rearrange("p (v t) -> p v t", t=SLOTS),
                turned[:].rearrange("p (t v) -> p v t", t=SLOTS)[:, 0:3, :],
            )
            give_bank("turn")
            for t in range(SLOTS):
                nc.scalar.activation(bt_rel[:, t : t + 1], bt_cols[:, t : t + 1], IDENTITY, scale=rel_cols[:, t : t + 1])

        picked = [held("picked%d" % a, [P, SLOTS, S], F32) for a in range(PASSES)]
        x_codes = [held("x_codes%d" % a, [P, S], U32) for a in range(PASSES)]
        x_scales = [held("x_scales%d" % a, [P, S], U8) for a in range(PASSES)]
        x_woven = held("x_woven", [P, S, SLOTS], BF16)
        x_woven_last = {}

        def gather(a, t, lo, hi):
            listed = offsets[:, lo * P // GROUP : hi * P // GROUP]
            nc.vector.tensor_tensor(
                picked[a][:, t, tiles(lo, hi)], planes[a][t][:].indirect(listed), weights[:, tiles(lo, hi)], MULT
            )

        def quantize_x(h):
            cols = tiles(*half(h))
            quantize(x_codes[0][:, cols], x_scales[0][:, cols], x_woven[:, cols, :])

        def interleave_x_last(copy, q):
            x_woven_last[q] = ring.tile([P, QUARTER * P, SLOTS], BF16, name="x_woven_last", align_bytes=64)
            interleave(copy, x_woven_last[q][:], picked[1][:, :, tiles(*quarter(q))])

        def quantize_x_last(q):
            cols = tiles(*quarter(q))
            quantize(x_codes[1][:, cols], x_scales[1][:, cols], x_woven_last[q][:])

        ws_codes = held("ws_codes", [P, PASSES * H * 2], U8)
        ws_scale = held("ws_scale", [P, PASSES * H], U8)

        def order_ws():
            for dst, src in ((ws_codes, ws_raw), (ws_scale, ws_scale_raw)):
                nc.vector.tensor_copy(
                    dst[:].bitcast(I32).rearrange("p (a t b w) -> p a t b w", a=PASSES, t=SLOTS, b=BLOCKS),
                    src[:].rearrange("p a (b t w) -> p a t b w", b=BLOCKS, t=SLOTS),
                )

        wt_woven = held("wt_woven", [P, PASSES * H, SLOTS], BF16)
        wt_codes = held("wt_codes", [P, PASSES * H], U32)
        wt_scale = held("wt_scale", [P, PASSES * H], U8)

        def cast_wt(a, b0, b1):
            by_slot = wt_raw[a][:].rearrange("p j (b t e) -> p t j b e", t=SLOTS, e=RUN)
            for t in range(SLOTS):
                first = a * H + t * P
                nc.scalar.copy(
                    wt_woven[:, first + b0 * RUN : first + b1 * RUN, :].rearrange(
                        "p (b u i) j -> p b u j i", u=RUN // LINE, i=LINE
                    ),
                    by_slot[:, t, :, b0:b1, :].rearrange("p j b (u i) -> p b u j i", i=LINE),
                )

        def quantize_wt(a):
            cols = slice(a * H, (a + 1) * H)
            quantize(wt_codes[:, cols], wt_scale[:, cols], wt_woven[:, cols, :])

        def source_pass(a, m):
            if a == 0:
                take_bank(("source", m))
            for t in range(SLOTS):
                u = a * SLOTS + t
                nc.tensor.matmul_mx(
                    out=bank_of(("source", m))[:, tiles(t, t + 1)],
                    lhsT=ws_codes[:, tiles(2 * u, 2 * u + 2)].bitcast(FP4X4),
                    lhsT_scale=ws_scale[:, tiles(u, u + 1)],
                    rhs=x_codes[a][:, tiles(m, m + 1)].bitcast(FP8X4),
                    rhs_scale=x_scales[a][:, tiles(m, m + 1)],
                    start=(a == 0 and t == 0),
                    stop=(a == PASSES - 1 and t == SLOTS - 1),
                )

        def target_sums(q, t):
            return bank_of(("target", q, t // 2))[:, tiles(*quarter(t % 2))]

        def target_pass(a, q):
            for t in range(SLOTS):
                if a == 0 and t % 2 == 0:
                    take_bank(("target", q, t // 2))
                u = a * SLOTS + t
                nc.tensor.matmul_mx(
                    out=target_sums(q, t),
                    lhsT=wt_codes[:, tiles(u, u + 1)].bitcast(FP8X4),
                    lhsT_scale=wt_scale[:, tiles(u, u + 1)],
                    rhs=x_codes[a][:, tiles(*quarter(q))].bitcast(FP8X4),
                    rhs_scale=x_scales[a][:, tiles(*quarter(q))],
                    start=(a == 0 and t % 2 == 0),
                    stop=(a == PASSES - 1 and t % 2 == 1),
                )

        hs_woven = held("hs_woven", [P, S, SLOTS], BF16)
        hs_codes = held("hs_codes", [P, S], U32)
        hs_scales = held("hs_scales", [P, S], U8)
        ht_flat = held("ht_flat", [P, SLOTS, S], BF16)
        ht_woven = held("ht_woven", [P, S, SLOTS], BF16)
        ht_codes = held("ht_codes", [P, S], U32)
        ht_scales = held("ht_scales", [P, S], U8)

        def empty_source(m):
            nc.vector.tensor_tensor(
                hs_woven[:, tiles(m, m + 1), :],
                bank_of(("source", m))[:].rearrange("p (t n) -> p n t", t=SLOTS),
                bs_cols.unsqueeze(1).to_broadcast([P, P, SLOTS]),
                ADD,
            )
            give_bank(("source", m))

        def quantize_source(lo, hi):
            quantize(hs_codes[:, tiles(lo, hi)], hs_scales[:, tiles(lo, hi)], hs_woven[:, tiles(lo, hi), :])

        def empty_target(q):
            for t in range(SLOTS):
                nc.scalar.activation(
                    ht_flat[:, t, tiles(*quarter(q))],
                    target_sums(q, t),
                    IDENTITY,
                    bias=bt_rel[:, t : t + 1],
                    scale=rel_cols[:, t : t + 1],
                )
            for pair in range(2):
                give_bank(("target", q, pair))

        def interleave_target(q):
            cols = tiles(*quarter(q))
            interleave(nc.vector.tensor_copy, ht_woven[:, cols, :], ht_flat[:, :, cols])

        def quantize_target(q):
            cols = tiles(*quarter(q))
            quantize(ht_codes[:, cols], ht_scales[:, cols], ht_woven[:, cols, :])

        def relu_on_scalar(dst, acc):
            nc.scalar.activation(dst, acc, RELU)

        def relu_on_vector(dst, acc):
            nc.vector.tensor_scalar(dst, acc, 0.0, None, MAX)

        def score_bank(user, sources, targets, relu, dst):
            acc = take_bank(user)
            width = targets[1] - targets[0]
            for u, m in enumerate(range(*sources)):
                nc.tensor.matmul_mx(
                    out=acc[:, tiles(u * width, (u + 1) * width)],
                    lhsT=hs_codes[:, tiles(m, m + 1)].bitcast(FP8X4),
                    lhsT_scale=hs_scales[:, tiles(m, m + 1)],
                    rhs=ht_codes[:, tiles(*targets)].bitcast(FP8X4),
                    rhs_scale=ht_scales[:, tiles(*targets)],
                    start=True,
                    stop=True,
                )
            relu(dst, acc[:])

        def score_block(sources, targets):
            result = narrow.tile([P, BANK], F32, name="result")
            score_bank("block", sources, targets, relu_on_scalar, result[:])
            give_bank("block")
            nc.sync.dma_start(
                out[tiles(*sources), tiles(*targets)].rearrange("(u p) j -> p u j", p=P),
                result[:].rearrange("p (u j) -> p u j", u=sources[1] - sources[0]),
            )

        def score_row(m, relus):
            row = wide.tile([P, S], F32, name="row")
            for h in range(2):
                score_bank(("row", h), (m, m + 1), half(h), relus[h], row[:, tiles(*half(h))])
            for h in range(2):
                give_bank(("row", h))
            nc.sync.dma_start(out[tiles(m, m + 1), :], row[:])

        for t in range(SLOTS):
            if t in (0, SLOTS - 1):
                for h in range(2):
                    gather(0, t, *half(h))
            else:
                gather(0, t, 0, TILES)
        turn_vectors()
        for h in range(2):
            cols = tiles(*half(h))
            interleave(nc.scalar.copy, x_woven[:, cols, :], picked[0][:, :, cols])
        gather(1, 0, 0, TILES)
        quantize_x(0)
        cast_wt(1, 0, BLOCKS)
        gather(1, 1, 0, TILES)
        quantize_x(1)
        quantize_wt(1)
        cast_wt(0, 0, BLOCKS // 2)
        gather(1, 2, 0, TILES)
        order_ws()
        cast_wt(0, BLOCKS // 2, BLOCKS)
        quantize_wt(0)

        for m in range(HALF):
            source_pass(0, m)
        for q in range(2):
            target_pass(0, q)

        for q in range(4):
            gather(1, SLOTS - 1, *quarter(q))
        for q in range(2):
            interleave_x_last(nc.scalar.copy, q)
        for q in range(2):
            quantize_x_last(q)
            target_pass(1, q)
            for m in range(*quarter(q)):
                source_pass(1, m)
            if q == 0:
                interleave_x_last(nc.scalar.copy, 2)
            empty_target(q)
        interleave_x_last(nc.vector.tensor_copy, 3)
        quantize_x_last(2)
        for a in range(PASSES):
            target_pass(a, 2)

        for m in range(*quarter(0)):
            empty_source(m)
        interleave_target(0)
        quantize_source(*quarter(0))
        quantize_target(0)
        score_block(quarter(0), quarter(0))
        quantize_x_last(3)
        for a in range(PASSES):
            target_pass(a, 3)
        interleave_target(1)
        quantize_target(1)
        score_block(quarter(0), quarter(1))
        empty_target(2)
        for m in range(*quarter(1)):
            empty_source(m)
            quantize_source(m, m + 1)
            score_block((m, m + 1), half(0))
        empty_target(3)
        for q in (2, 3):
            if q == 2:
                for m in range(*quarter(q)):
                    for a in range(PASSES):
                        source_pass(a, m)
            interleave_target(q)
            quantize_target(q)
            for source_q in range(2):
                score_block(quarter(source_q), quarter(q))
            if q == 2:
                for m in range(*quarter(3)):
                    for a in range(PASSES):
                        source_pass(a, m)
        empty_source(HALF)
        quantize_source(HALF, HALF + 1)
        for h in range(2):
            score_block((HALF, HALF + 1), half(h))
        last_rows = range(HALF + 1, TILES)
        for m in last_rows:
            empty_source(m)
            quantize_source(m, m + 1)
        last_relus = ((relu_on_scalar, relu_on_scalar), (relu_on_vector, relu_on_vector), (relu_on_scalar, relu_on_vector))
        for m, relus in zip(last_rows, last_relus):
            score_row(m, relus)
